import numpy as np
import ml_dtypes


def mxq(x, axis, fmt="e4m3"):
    dtype, down = {"e4m3": (ml_dtypes.float8_e4m3fn, 7), "e5m2": (ml_dtypes.float8_e5m2, 14)}[fmt]
    v = np.moveaxis(np.asarray(x, np.float32).astype(ml_dtypes.bfloat16).astype(np.float64), axis, -1)
    blocks = v.reshape(v.shape[:-1] + (-1, 32))
    amax = np.abs(blocks).max(-1, keepdims=True)
    byte = np.maximum(np.where(amax > 0, np.frexp(amax)[1] - 1 + 127, 0) - down, 1)
    scale = np.exp2(byte - 127.0)
    codes = (blocks / scale).astype(np.float32).astype(dtype).astype(np.float64)
    return np.moveaxis((codes * scale).reshape(v.shape), -1, axis)


WIDE = False


def mx_kscale(k):
    if not WIDE:
        return np.ones(k)
    levels = np.array([10, -10, 5, -5, 0])
    if k % 512:
        return np.exp2(np.random.permutation(np.resize(levels, k // 32))).repeat(32)
    a = np.empty((k // 512, 16))
    for p in range(k // 512):
        a[p, :8] = np.random.permutation(np.resize(levels, 8))
        for g in range(8):
            far = levels[np.abs(levels - a[p, g]) >= 10]
            a[p, g + 8] = far[np.random.randint(len(far))]
    return np.exp2(a.ravel()).repeat(32)


BF16 = ml_dtypes.bfloat16


def bf(x):
    return np.asarray(x, np.float32).astype(BF16)


def f64(x):
    return np.asarray(x).astype(np.float64)

def planes(Y):
    n, m = Y.shape
    b = f64(bf(Y)).reshape(n // 32, 32, m)
    amax = np.abs(b).max(1)
    byte = np.clip(np.where(amax > 0, np.frexp(amax)[1] - 1 + 127 - 7, 1), 1, 254)
    codes = (b * np.exp2(127.0 - byte)[:, None, :]).reshape(n, m).astype(np.float32).astype(ml_dtypes.float8_e4m3fn).view(np.uint8)
    words = codes.reshape(n // 512, 128, 4, m).transpose(0, 1, 3, 2)
    return np.ascontiguousarray(words), np.ascontiguousarray(byte.astype(np.uint8).reshape(n // 512, 16, m))


K, N, M, C, Z = 4, 1024, 1024, 512, 512


def log_sum_exp_last(f):
    top = np.max(f, axis=-1, keepdims=True)
    total = np.sum(np.exp(f - top), axis=-1)
    return np.log(total) + np.squeeze(top, axis=-1)


def setup_inputs():
    s, t = mx_kscale(C), mx_kscale(Z)
    return {"c": bf(np.random.standard_normal((N, C)) * s),
            "w": bf(np.random.standard_normal((K, C, Z)) / np.sqrt(C) / s[None, :, None] * t),
            "z": bf(1.5 * np.random.standard_normal((K, M, Z)) / np.sqrt(Z) / t)}


def core(c, w, z):
    num_candidates = z.shape[1]
    p = mxq(f64(c), 1, "e4m3") @ mxq(f64(w), 1, "e4m3")
    f = mxq(p, 2, "e4m3") @ mxq(f64(z), 2, "e4m3").transpose(0, 2, 1)
    l = log_sum_exp_last(f) - np.log(num_candidates)
    r = f - l[:, :, None]
    return r


def reference(c, w, z):
    R_out = core(c, w, z)
    words, scales = planes(np.moveaxis(R_out, 1, 0).reshape(1024, -1))
    return R_out, words, scales

@@ -1,0 +1,347 @@
+import math
+from contextlib import ExitStack
+
+import concourse.mybir as mybir
+from concourse.masks import make_identity
+
+STEPS, N, M, C, Z = 4, 1024, 1024, 512, 512
+FLOPS = 2 * STEPS * N * Z * (C + M)
+
+F32 = mybir.dt.float32
+BF16 = mybir.dt.bfloat16
+I32 = mybir.dt.int32
+U32 = mybir.dt.uint32
+U8 = mybir.dt.uint8
+FP8X4 = mybir.dt.float8_e4m3fn_x4
+ALU = mybir.AluOpType
+ACT = mybir.ActivationFunctionType
+
+P = 128
+HALF = 512
+TILES = STEPS * 8
+GROUPS = STEPS * 2
+
+LN2 = math.log(2.0)
+ROOT = 64
+REACH = 2.0 ** (5.0 / ROOT) - 1.0
+LOG_SERIES = (
+    1.0 + REACH**6 / 64.0,
+    -1.0 / 2.0,
+    1.0 / 3.0 - REACH**4 / 8.0,
+    -1.0 / 4.0,
+    1.0 / 5.0 + REACH**2 / 4.0,
+    -1.0 / 6.0,
+)
+
+
+def tile_cpclogdensityratiomatrix_x1_kernel(tc, c, w, z, out_0, out_1, out_2):
+    nc = tc.nc
+    with ExitStack() as ctx:
+        keep = ctx.enter_context(tc.tile_pool(name="keep", bufs=1))
+        work = ctx.enter_context(tc.tile_pool(name="work", bufs=2))
+        psum = ctx.enter_context(tc.psum_pool(name="psum", bufs=2))
+
+        ident = keep.tile([P, P], F32, name="ident")
+        make_identity(nc, ident[:])
+        root = keep.tile([P, 4], F32, name="root")
+        nc.gpsimd.memset(root[:], 1.0 / ROOT)
+
+        c_codes = keep.tile([P, N], U32, name="c_codes", align_bytes=64)
+        c_scales = keep.tile([P, N], U8, name="c_scales", align_bytes=64)
+        c_raw, w_raw, z_raw = {}, {}, {}
+        w_codes, w_scales, z_codes, z_scales = {}, {}, {}, {}
+        turned, grouped, latent, lat_bf, lat_codes, lat_scales, w_grouped = {}, {}, {}, {}, {}, {}, {}
+        scores, neg_f, first_min, neg_max, sums, shift = {}, {}, {}, {}, {}, {}
+        packed, out_codes, out_scales = {}, {}, {}
+
+        def load_c(g, parts):
+            c_raw[g] = keep.tile([P, 4, C], BF16, name="c_raw%d" % g)
+            src = c[512 * g : 512 * (g + 1), :].rearrange("(j t) k -> j t k", t=4)
+            for t0 in range(0, 4, 4 // parts):
+                sl = slice(t0, t0 + 4 // parts)
+                nc.sync.dma_start(out=c_raw[g][:, sl, :], in_=src[:, sl, :])
+
+        def load_w(k):
+            w_raw[k] = keep.tile([P, 4, Z], BF16, name="w_raw%d" % k)
+            nc.sync.dma_start(out=w_raw[k][:], in_=w[k].rearrange("(p j) z -> p j z", j=4))
+
+        def load_z(k):
+            z_raw[k] = keep.tile([P, 8, Z], BF16, name="z_raw%d" % k)
+            src = z[k].rearrange("(r j) z -> j r z", j=P)
+            for r0 in (0, 4):
+                nc.sync.dma_start(out=z_raw[k][:, r0 : r0 + 4, :], in_=src[:, r0 : r0 + 4, :])
+
+        def turn(key):
+            kind, i, b = key
+            raw = c_raw[i] if kind == "c" else z_raw[i]
+            bank = psum.tile([P, 2, 2, P], F32, name="turned", bufs=2)
+            for s in range(2):
+                words = raw[:, 2 * b + s, :].bitcast(F32)
+                for u in range(2):
+                    nc.tensor.transpose(bank[:, s, u, :], words[:, u : 256 : 2], ident[:])
+            turned[key] = bank
+
+        def gather(key, copy):
+            grouped[key] = work.tile([P, 256, 4], BF16, name="grouped", bufs=4, align_bytes=64)
+            dst = grouped[key][:].rearrange("p n f -> p (n f)").bitcast(F32)
+            copy(
+                out=dst.rearrange("p (s r u) -> p s r u", s=2, u=2),
+                in_=turned.pop(key)[:].rearrange("p s u r -> p s r u"),
+            )
+
+        def quantise_turned(key):
+            kind, i, b = key
+            if kind == "c":
+                codes, scales, at = c_codes, c_scales, 512 * i + 256 * b
+            else:
+                if b == 0:
+                    z_codes[i] = work.tile([P, M], U32, name="z_codes", bufs=2, align_bytes=64)
+                    z_scales[i] = work.tile([P, M], U8, name="z_scales", bufs=2, align_bytes=64)
+                codes, scales, at = z_codes[i], z_scales[i], 256 * b
+            nc.vector.quantize_mx(
+                out=codes[:, at : at + 256].bitcast(FP8X4),
+                scales=scales[:, at : at + 256],
+                in_=grouped.pop(key)[:].rearrange("p n f -> p (n f)"),
+            )
+
+        def lay_w(k, t0, t1):
+            if t0 == 0:
+                w_grouped[k] = work.tile([P, 4 * Z], BF16, name="w_grouped", bufs=2, align_bytes=64)
+            nc.vector.tensor_copy(
+                out=w_grouped[k][:].rearrange("p (t m j) -> p t m j", t=4, j=4)[:, t0:t1],
+                in_=w_raw[k][:].rearrange("p j (m t) -> p t m j", t=4)[:, t0:t1],
+            )
+
+        def quantise_w(k):
+            w_codes[k] = work.tile([P, Z], U32, name="w_codes", bufs=2, align_bytes=64)
+            w_scales[k] = work.tile([P, Z], U8, name="w_scales", bufs=2, align_bytes=64)
+            nc.vector.quantize_mx(out=w_codes[k][:].bitcast(FP8X4), scales=w_scales[k][:], in_=w_grouped[k][:])
+
+        def multiply_latent(s):
+            k, rest = divmod(s, 8)
+            bank = psum.tile([P, 4, P], F32, name="latent", bufs=2)
+            cols = slice(P * rest, P * (rest + 1))
+            for t in range(4):
+                wc = slice(P * t, P * (t + 1))
+                nc.tensor.matmul_mx(
+                    out=bank[:, t, :],
+                    lhsT=w_codes[k][:, wc].bitcast(FP8X4),
+                    lhsT_scale=w_scales[k][:, wc],
+                    rhs=c_codes[:, cols].bitcast(FP8X4),
+                    rhs_scale=c_scales[:, cols],
+                    start=True,
+                    stop=True,
+                )
+            latent[s] = bank
+
+        def round_latent(s):
+            lat_bf[s] = work.tile([P, P, 4], BF16, name="lat_bf", bufs=4, align_bytes=64)
+            nc.scalar.copy(out=lat_bf[s][:], in_=latent.pop(s)[:].rearrange("p t j -> p j t"))
+
+        def quantise_latent(s):
+            lat_codes[s] = work.tile([P, P], U32, name="lat_codes", bufs=4, align_bytes=64)
+            lat_scales[s] = work.tile([P, P], U8, name="lat_scales", bufs=4, align_bytes=64)
+            nc.vector.quantize_mx(
+                out=lat_codes[s][:].bitcast(FP8X4),
+                scales=lat_scales[s][:],
+                in_=lat_bf.pop(s)[:].rearrange("p j t -> p (j t)"),
+            )
+
+        def multiply_scores(s):
+            k = s // 8
+            for h in range(2):
+                bank = psum.tile([P, HALF], F32, name="scores", bufs=4)
+                cols = slice(HALF * h, HALF * (h + 1))
+                nc.tensor.matmul_mx(
+                    out=bank[:],
+                    lhsT=lat_codes[s][:].bitcast(FP8X4),
+                    lhsT_scale=lat_scales[s][:],
+                    rhs=z_codes[k][:, cols].bitcast(FP8X4),
+                    rhs_scale=z_scales[k][:, cols],
+                    start=True,
+                    stop=True,
+                )
+                scores[s, h] = bank
+
+        def negate_and_min(s, h):
+            i, t = divmod(s, 4)
+            if t == 0 and h == 0:
+                neg_f[i] = work.tile([P, 4, M], F32, name="neg_f", bufs=4, align_bytes=64)
+                first_min[i] = work.tile([P, 4], F32, name="first_min", bufs=2)
+                neg_max[i] = work.tile([P, 4], F32, name="neg_max", bufs=3)
+                sums[i] = work.tile([P, 4], F32, name="sums", bufs=3)
+            nc.vector.tensor_scalar(
+                out=neg_f[i][:, t, HALF * h : HALF * (h + 1)],
+                in0=scores.pop((s, h))[:],
+                scalar1=-1.0,
+                scalar2=None if h == 0 else first_min[i][:, t : t + 1],
+                op0=ALU.mult,
+                op1=ALU.min,
+                accum_out=(first_min if h == 0 else neg_max)[i][:, t : t + 1],
+            )
+
+        def exponentiate(s):
+            i, t = divmod(s, 4)
+            exps = work.tile([P, M], BF16, name="exps", bufs=2)
+            nc.scalar.activation(
+                out=exps[:],
+                in_=neg_f[i][:, t, :],
+                func=ACT.Exp,
+                scale=-1.0,
+                bias=neg_max[i][:, t : t + 1],
+                accum_out=sums[i][:, t : t + 1],
+            )
+
+        def finish_log(i):
+            u = work.tile([P, 4], F32, name="u", bufs=2)
+            h = work.tile([P, 4], F32, name="h", bufs=2)
+            shift[i] = work.tile([P, 4], F32, name="shift", bufs=3)
+            eng = nc.gpsimd
+
+            def affine(out, in_, mul, add):
+                eng.tensor_scalar(out=out[:], in0=in_[:], scalar1=mul, scalar2=add, op0=ALU.mult, op1=ALU.add)
+
+            def two(out, a, b, op):
+                eng.tensor_tensor(out=out[:], in0=a[:], in1=b[:], op=op)
+
+            two(u, sums[i], root, ALU.pow)
+            affine(u, u, 2.0 ** (-5.0 / ROOT), -1.0)
+            affine(h, u, LOG_SERIES[5], LOG_SERIES[4])
+            for coefficient in reversed(LOG_SERIES[:4]):
+                two(h, h, u, ALU.mult)
+                affine(h, h, 1.0, coefficient)
+            two(h, h, u, ALU.mult)
+            affine(h, h, -float(ROOT), math.log(M) - 5.0 * LN2)
+            two(shift[i], neg_max[i], h, ALU.add)
+
+        def subtract(i, t, engine):
+            row = neg_f[i][:, t, :]
+            sh = shift[i][:, t : t + 1]
+            if engine == "scalar":
+                nc.scalar.activation(out=row, in_=row, func=ACT.Identity, scale=-1.0, bias=sh)
+            else:
+                nc.vector.tensor_scalar(out=row, in0=row, scalar1=-1.0, scalar2=sh, op0=ALU.mult, op1=ALU.add)
+            k, g = divmod(i, 2)
+            dst = out_0[k, 512 * g : 512 * (g + 1), :].rearrange("(p t) m -> p t m", t=4)
+            nc.sync.dma_start(out=dst[:, t, :], in_=row)
+
+        def pack(i, h):
+            packed[i, h] = work.tile([P, HALF, 4], BF16, name="packed", bufs=3, align_bytes=64)
+            nc.vector.tensor_copy(
+                out=packed[i, h][:],
+                in_=neg_f[i][:, :, HALF * h : HALF * (h + 1)].rearrange("p t m -> p m t"),
+            )
+
+        def quantise_out(i, h):
+            k, g = divmod(i, 2)
+            if h == 0:
+                out_scales[i] = work.tile([P, M], U8, name="out_scales", bufs=3, align_bytes=64)
+            out_codes[i] = work.tile([P, HALF], U32, name="out_codes", bufs=4, align_bytes=64)
+            nc.vector.quantize_mx(
+                out=out_codes[i][:].bitcast(FP8X4),
+                scales=out_scales[i][:, HALF * h : HALF * (h + 1)],
+                in_=packed.pop((i, h))[:].rearrange("p m t -> p (m t)"),
+            )
+            m0 = M * k + HALF * h
+            dst = out_1[g, :, m0 : m0 + HALF, :].rearrange("p m b -> p (m b)")
+            nc.sync.dma_start(out=dst.bitcast(I32), in_=out_codes[i][:].bitcast(I32))
+            if h == 1:
+                for quad in range(4):
+                    dst = out_2[g, 4 * quad : 4 * quad + 4, M * k : M * (k + 1)]
+                    nc.sync.dma_start(
+                        out=dst.bitcast(I32), in_=out_scales[i][32 * quad : 32 * quad + 4, :].bitcast(I32)
+                    )
+
+        with tc.manual_schedule():
+            load_c(0, 2)
+            load_w(0)
+            load_z(0)
+            load_c(1, 1)
+            for k in range(1, STEPS):
+                load_w(k)
+                load_z(k)
+
+            turn(("c", 0, 0))
+            turn(("c", 0, 1))
+            gather(("c", 0, 0), nc.scalar.copy)
+            gather(("c", 0, 1), nc.vector.tensor_copy)
+            quantise_turned(("c", 0, 0))
+            quantise_turned(("c", 0, 1))
+            lay_w(0, 0, 4)
+            turn(("z", 0, 0))
+            gather(("z", 0, 0), nc.scalar.copy)
+            quantise_w(0)
+            multiply_latent(0)
+            round_latent(0)
+            turn(("z", 0, 1))
+            gather(("z", 0, 1), nc.vector.tensor_copy)
+            multiply_latent(1)
+            round_latent(1)
+            quantise_turned(("z", 0, 0))
+            quantise_turned(("z", 0, 1))
+            turn(("z", 0, 2))
+            gather(("z", 0, 2), nc.scalar.copy)
+            quantise_latent(0)
+            turn(("z", 0, 3))
+            gather(("z", 0, 3), nc.vector.tensor_copy)
+            multiply_latent(2)
+            round_latent(2)
+            quantise_turned(("z", 0, 2))
+            quantise_turned(("z", 0, 3))
+            quantise_latent(1)
+            multiply_scores(0)
+
+            for s in range(TILES + 12):
+                k, loc = divmod(s, 8)
+                banks = []
+                if s == 0:
+                    banks = [("c", 1, 0), ("c", 1, 1)]
+                elif k + 1 < STEPS and 2 <= loc < 6:
+                    banks = [("z", k + 1, loc - 2)]
+                for key in banks:
+                    turn(key)
+                if s + 3 < TILES:
+                    multiply_latent(s + 3)
+                if s + 1 < TILES:
+                    multiply_scores(s + 1)
+
+                if 1 <= s <= TILES:
+                    exponentiate(s - 1)
+                i, r = divmod(s - 4, 4)
+                if r == 0 and 0 <= i < GROUPS:
+                    finish_log(i)
+                for key in banks:
+                    gather(key, nc.scalar.copy)
+                if s + 3 < TILES:
+                    round_latent(s + 3)
+
+                if s < TILES:
+                    negate_and_min(s, 0)
+                if s + 2 < TILES:
+                    quantise_latent(s + 2)
+                if s < TILES:
+                    negate_and_min(s, 1)
+                if s == 0:
+                    for key in banks:
+                        quantise_turned(key)
+                if k + 1 < STEPS:
+                    if loc < 2:
+                        lay_w(k + 1, 2 * loc, 2 * loc + 2)
+                    if loc == 2:
+                        quantise_w(k + 1)
+                    if 3 <= loc < 7:
+                        quantise_turned(("z", k + 1, loc - 3))
+                i, r = divmod(s - 6, 4)
+                if 0 <= i < GROUPS:
+                    if r == 0:
+                        subtract(i, 0, "vector")
+                        subtract(i, 1, "scalar")
+                    if r == 1:
+                        subtract(i, 2, "scalar")
+                        subtract(i, 3, "scalar")
+                i, r = divmod(s - 8, 4)
+                if 0 <= i < GROUPS and r in (0, 2):
+                    pack(i, r // 2)
+                i, r = divmod(s - 9, 4)
+                if 0 <= i < GROUPS and r in (0, 2):
+                    quantise_out(i, r // 2)

@@ -51,7 +51,7 @@ def tile_cpclogdensityratiomatrix_x1_kernel(tc, c, w, z, out_0, out_1, out_2):
         c_raw, w_raw, z_raw = {}, {}, {}
         w_codes, w_scales, z_codes, z_scales = {}, {}, {}, {}
         turned, grouped, latent, lat_bf, lat_codes, lat_scales, w_grouped = {}, {}, {}, {}, {}, {}, {}
-        scores, neg_f, first_min, neg_max, sums, shift = {}, {}, {}, {}, {}, {}
+        scores, neg_f, first_min, neg_max, sums, shift, roots = {}, {}, {}, {}, {}, {}, {}
         packed, out_codes, out_scales = {}, {}, {}
 
         def load_c(g, parts):
@@ -192,27 +192,43 @@ def tile_cpclogdensityratiomatrix_x1_kernel(tc, c, w, z, out_0, out_1, out_2):
                 accum_out=sums[i][:, t : t + 1],
             )
 
-        def finish_log(i):
+        def take_root(i):
+            roots[i] = work.tile([P, 4], F32, name="roots", bufs=2)
+            nc.gpsimd.tensor_tensor(out=roots[i][:], in0=sums[i][:], in1=root[:], op=ALU.pow)
+
+        def affine(eng, out, in_, mul, add):
+            eng.tensor_scalar(out=out[:], in0=in_[:], scalar1=mul, scalar2=add, op0=ALU.mult, op1=ALU.add)
+
+        def finish_log(i, eng):
             u = work.tile([P, 4], F32, name="u", bufs=2)
             h = work.tile([P, 4], F32, name="h", bufs=2)
             shift[i] = work.tile([P, 4], F32, name="shift", bufs=3)
-            eng = nc.gpsimd
-
-            def affine(out, in_, mul, add):
-                eng.tensor_scalar(out=out[:], in0=in_[:], scalar1=mul, scalar2=add, op0=ALU.mult, op1=ALU.add)
-
-            def two(out, a, b, op):
-                eng.tensor_tensor(out=out[:], in0=a[:], in1=b[:], op=op)
-
-            two(u, sums[i], root, ALU.pow)
-            affine(u, u, 2.0 ** (-5.0 / ROOT), -1.0)
-            affine(h, u, LOG_SERIES[5], LOG_SERIES[4])
+            base = work.tile([P, 4], F32, name="base", bufs=2)
+            affine(eng, base, neg_max[i], 1.0, math.log(M) - 5.0 * LN2)
+            affine(eng, u, roots[i], 2.0 ** (-5.0 / ROOT), -1.0)
+            affine(eng, h, u, LOG_SERIES[5], LOG_SERIES[4])
             for coefficient in reversed(LOG_SERIES[:4]):
-                two(h, h, u, ALU.mult)
-                affine(h, h, 1.0, coefficient)
-            two(h, h, u, ALU.mult)
-            affine(h, h, -float(ROOT), math.log(M) - 5.0 * LN2)
-            two(shift[i], neg_max[i], h, ALU.add)
+                eng.tensor_tensor(out=h[:], in0=h[:], in1=u[:], op=ALU.mult)
+                affine(eng, h, h, 1.0, coefficient)
+            eng.tensor_tensor(out=h[:], in0=h[:], in1=u[:], op=ALU.mult)
+            affine(eng, h, h, -float(ROOT), 0.0)
+            eng.tensor_tensor(out=shift[i][:], in0=base[:], in1=h[:], op=ALU.add)
+
+        def finish_log_on_vector(i):
+            u = work.tile([P, 4], F32, name="u", bufs=2)
+            h = work.tile([P, 4], F32, name="h", bufs=2)
+            shift[i] = work.tile([P, 4], F32, name="shift", bufs=3)
+            base = work.tile([P, 4], F32, name="base", bufs=2)
+            affine(nc.vector, base, neg_max[i], 1.0, math.log(M) - 5.0 * LN2)
+            affine(nc.vector, u, roots[i], 2.0 ** (-5.0 / ROOT), -1.0)
+            affine(nc.vector, h, u, LOG_SERIES[5], 0.0)
+            for coefficient in reversed(LOG_SERIES[:5]):
+                nc.vector.scalar_tensor_tensor(
+                    out=h[:], in0=h[:], scalar=coefficient, in1=u[:], op0=ALU.add, op1=ALU.mult
+                )
+            nc.vector.scalar_tensor_tensor(
+                out=shift[i][:], in0=h[:], scalar=-float(ROOT), in1=base[:], op0=ALU.mult, op1=ALU.add
+            )
 
         def subtract(i, t, engine):
             row = neg_f[i][:, t, :]
@@ -291,7 +307,7 @@ def tile_cpclogdensityratiomatrix_x1_kernel(tc, c, w, z, out_0, out_1, out_2):
             quantise_latent(1)
             multiply_scores(0)
 
-            for s in range(TILES + 12):
+            for s in range(TILES):
                 k, loc = divmod(s, 8)
                 banks = []
                 if s == 0:
@@ -309,7 +325,8 @@ def tile_cpclogdensityratiomatrix_x1_kernel(tc, c, w, z, out_0, out_1, out_2):
                     exponentiate(s - 1)
                 i, r = divmod(s - 4, 4)
                 if r == 0 and 0 <= i < GROUPS:
-                    finish_log(i)
+                    take_root(i)
+                    finish_log(i, nc.gpsimd)
                 for key in banks:
                     gather(key, nc.scalar.copy)
                 if s + 3 < TILES:
@@ -331,7 +348,7 @@ def tile_cpclogdensityratiomatrix_x1_kernel(tc, c, w, z, out_0, out_1, out_2):
                         quantise_w(k + 1)
                     if 3 <= loc < 7:
                         quantise_turned(("z", k + 1, loc - 3))
-                i, r = divmod(s - 6, 4)
+                i, r = divmod(s - 8, 4)
                 if 0 <= i < GROUPS:
                     if r == 0:
                         subtract(i, 0, "vector")
@@ -339,9 +356,32 @@ def tile_cpclogdensityratiomatrix_x1_kernel(tc, c, w, z, out_0, out_1, out_2):
                     if r == 1:
                         subtract(i, 2, "scalar")
                         subtract(i, 3, "scalar")
-                i, r = divmod(s - 8, 4)
+                i, r = divmod(s - 10, 4)
                 if 0 <= i < GROUPS and r in (0, 2):
                     pack(i, r // 2)
-                i, r = divmod(s - 9, 4)
+                i, r = divmod(s - 11, 4)
                 if 0 <= i < GROUPS and r in (0, 2):
                     quantise_out(i, r // 2)
+
+            last = GROUPS - 1
+            exponentiate(TILES - 1)
+            take_root(last)
+            pack(last - 2, 1)
+            subtract(last - 1, 0, "vector")
+            subtract(last - 1, 1, "scalar")
+            subtract(last - 1, 2, "scalar")
+            subtract(last - 1, 3, "vector")
+            quantise_out(last - 2, 1)
+            finish_log_on_vector(last)
+            pack(last - 1, 0)
+            subtract(last, 2, "scalar")
+            subtract(last, 3, "scalar")
+            subtract(last, 0, "vector")
+            subtract(last, 1, "vector")
+            quantise_out(last - 1, 0)
+            pack(last - 1, 1)
+            pack(last, 0)
+            quantise_out(last - 1, 1)
+            quantise_out(last, 0)
+            pack(last, 1)
+            quantise_out(last, 1)

@@ -21,17 +21,8 @@ HALF = 512
 TILES = STEPS * 8
 GROUPS = STEPS * 2
 
-LN2 = math.log(2.0)
-ROOT = 64
-REACH = 2.0 ** (5.0 / ROOT) - 1.0
-LOG_SERIES = (
-    1.0 + REACH**6 / 64.0,
-    -1.0 / 2.0,
-    1.0 / 3.0 - REACH**4 / 8.0,
-    -1.0 / 4.0,
-    1.0 / 5.0 + REACH**2 / 4.0,
-    -1.0 / 6.0,
-)
+ROOT = 512
+CENTRE = 3.5
 
 
 def tile_cpclogdensityratiomatrix_x1_kernel(tc, c, w, z, out_0, out_1, out_2):
@@ -45,25 +36,30 @@ def tile_cpclogdensityratiomatrix_x1_kernel(tc, c, w, z, out_0, out_1, out_2):
         make_identity(nc, ident[:])
         root = keep.tile([P, 4], F32, name="root")
         nc.gpsimd.memset(root[:], 1.0 / ROOT)
+        minus_two = keep.tile([P, 1], F32, name="minus_two")
+        nc.gpsimd.memset(minus_two[:], -2.0)
+        guess_bias = keep.tile([P, 1], F32, name="guess_bias")
+        nc.gpsimd.memset(guess_bias[:], -ROOT / 2.0 - CENTRE)
 
         c_codes = keep.tile([P, N], U32, name="c_codes", align_bytes=64)
         c_scales = keep.tile([P, N], U8, name="c_scales", align_bytes=64)
         c_raw, w_raw, z_raw = {}, {}, {}
         w_codes, w_scales, z_codes, z_scales = {}, {}, {}, {}
         turned, grouped, latent, lat_bf, lat_codes, lat_scales, w_grouped = {}, {}, {}, {}, {}, {}, {}
-        scores, neg_f, first_min, neg_max, sums, shift, roots = {}, {}, {}, {}, {}, {}, {}
+        scores, neg_f, first_min, neg_max, sums, shift, roots, squares, ratios = {}, {}, {}, {}, {}, {}, {}, {}, {}
         packed, out_codes, out_scales = {}, {}, {}
 
-        def load_c(g, parts):
-            c_raw[g] = keep.tile([P, 4, C], BF16, name="c_raw%d" % g)
+        def load_c(g, t0, t1):
+            if t0 == 0:
+                c_raw[g] = keep.tile([P, 4, C], BF16, name="c_raw%d" % g)
             src = c[512 * g : 512 * (g + 1), :].rearrange("(j t) k -> j t k", t=4)
-            for t0 in range(0, 4, 4 // parts):
-                sl = slice(t0, t0 + 4 // parts)
-                nc.sync.dma_start(out=c_raw[g][:, sl, :], in_=src[:, sl, :])
+            nc.sync.dma_start(out=c_raw[g][:, t0:t1, :], in_=src[:, t0:t1, :])
 
-        def load_w(k):
-            w_raw[k] = keep.tile([P, 4, Z], BF16, name="w_raw%d" % k)
-            nc.sync.dma_start(out=w_raw[k][:], in_=w[k].rearrange("(p j) z -> p j z", j=4))
+        def load_w(k, z0, z1):
+            if z0 == 0:
+                w_raw[k] = keep.tile([P, 4, Z], BF16, name="w_raw%d" % k)
+            src = w[k].rearrange("(p j) z -> p j z", j=4)
+            nc.sync.dma_start(out=w_raw[k][:, :, z0:z1], in_=src[:, :, z0:z1])
 
         def load_z(k):
             z_raw[k] = keep.tile([P, 8, Z], BF16, name="z_raw%d" % k)
@@ -104,12 +100,13 @@ def tile_cpclogdensityratiomatrix_x1_kernel(tc, c, w, z, out_0, out_1, out_2):
                 in_=grouped.pop(key)[:].rearrange("p n f -> p (n f)"),
             )
 
-        def lay_w(k, t0, t1):
-            if t0 == 0:
+        def lay_w(k, half):
+            if half == 0:
                 w_grouped[k] = work.tile([P, 4 * Z], BF16, name="w_grouped", bufs=2, align_bytes=64)
+            ms = slice(64 * half, 64 * half + 64)
             nc.vector.tensor_copy(
-                out=w_grouped[k][:].rearrange("p (t m j) -> p t m j", t=4, j=4)[:, t0:t1],
-                in_=w_raw[k][:].rearrange("p j (m t) -> p t m j", t=4)[:, t0:t1],
+                out=w_grouped[k][:].rearrange("p (t m j) -> p t m j", t=4, j=4)[:, :, ms],
+                in_=w_raw[k][:].rearrange("p j (m t) -> p t m j", t=4)[:, :, ms],
             )
 
         def quantise_w(k):
@@ -147,21 +144,20 @@ def tile_cpclogdensityratiomatrix_x1_kernel(tc, c, w, z, out_0, out_1, out_2):
                 in_=lat_bf.pop(s)[:].rearrange("p j t -> p (j t)"),
             )
 
-        def multiply_scores(s):
+        def multiply_scores(s, h):
             k = s // 8
-            for h in range(2):
-                bank = psum.tile([P, HALF], F32, name="scores", bufs=4)
-                cols = slice(HALF * h, HALF * (h + 1))
-                nc.tensor.matmul_mx(
-                    out=bank[:],
-                    lhsT=lat_codes[s][:].bitcast(FP8X4),
-                    lhsT_scale=lat_scales[s][:],
-                    rhs=z_codes[k][:, cols].bitcast(FP8X4),
-                    rhs_scale=z_scales[k][:, cols],
-                    start=True,
-                    stop=True,
-                )
-                scores[s, h] = bank
+            bank = psum.tile([P, HALF], F32, name="scores", bufs=4)
+            cols = slice(HALF * h, HALF * (h + 1))
+            nc.tensor.matmul_mx(
+                out=bank[:],
+                lhsT=lat_codes[s][:].bitcast(FP8X4),
+                lhsT_scale=lat_scales[s][:],
+                rhs=z_codes[k][:, cols].bitcast(FP8X4),
+                rhs_scale=z_scales[k][:, cols],
+                start=True,
+                stop=True,
+            )
+            scores[s, h] = bank
 
         def negate_and_min(s, h):
             i, t = divmod(s, 4)
@@ -196,39 +192,32 @@ def tile_cpclogdensityratiomatrix_x1_kernel(tc, c, w, z, out_0, out_1, out_2):
             roots[i] = work.tile([P, 4], F32, name="roots", bufs=2)
             nc.gpsimd.tensor_tensor(out=roots[i][:], in0=sums[i][:], in1=root[:], op=ALU.pow)
 
-        def affine(eng, out, in_, mul, add):
-            eng.tensor_scalar(out=out[:], in0=in_[:], scalar1=mul, scalar2=add, op0=ALU.mult, op1=ALU.add)
-
-        def finish_log(i, eng):
-            u = work.tile([P, 4], F32, name="u", bufs=2)
-            h = work.tile([P, 4], F32, name="h", bufs=2)
-            shift[i] = work.tile([P, 4], F32, name="shift", bufs=3)
-            base = work.tile([P, 4], F32, name="base", bufs=2)
-            affine(eng, base, neg_max[i], 1.0, math.log(M) - 5.0 * LN2)
-            affine(eng, u, roots[i], 2.0 ** (-5.0 / ROOT), -1.0)
-            affine(eng, h, u, LOG_SERIES[5], LOG_SERIES[4])
-            for coefficient in reversed(LOG_SERIES[:4]):
-                eng.tensor_tensor(out=h[:], in0=h[:], in1=u[:], op=ALU.mult)
-                affine(eng, h, h, 1.0, coefficient)
-            eng.tensor_tensor(out=h[:], in0=h[:], in1=u[:], op=ALU.mult)
-            affine(eng, h, h, -float(ROOT), 0.0)
-            eng.tensor_tensor(out=shift[i][:], in0=base[:], in1=h[:], op=ALU.add)
-
-        def finish_log_on_vector(i):
-            u = work.tile([P, 4], F32, name="u", bufs=2)
-            h = work.tile([P, 4], F32, name="h", bufs=2)
-            shift[i] = work.tile([P, 4], F32, name="shift", bufs=3)
-            base = work.tile([P, 4], F32, name="base", bufs=2)
-            affine(nc.vector, base, neg_max[i], 1.0, math.log(M) - 5.0 * LN2)
-            affine(nc.vector, u, roots[i], 2.0 ** (-5.0 / ROOT), -1.0)
-            affine(nc.vector, h, u, LOG_SERIES[5], 0.0)
-            for coefficient in reversed(LOG_SERIES[:5]):
-                nc.vector.scalar_tensor_tensor(
-                    out=h[:], in0=h[:], scalar=coefficient, in1=u[:], op0=ALU.add, op1=ALU.mult
-                )
-            nc.vector.scalar_tensor_tensor(
-                out=shift[i][:], in0=h[:], scalar=-float(ROOT), in1=base[:], op0=ALU.mult, op1=ALU.add
+        def guess_log(i):
+            squares[i] = work.tile([P, 4], F32, name="squares", bufs=2)
+            ratios[i] = work.tile([P, 4], F32, name="ratios", bufs=2)
+            nc.scalar.activation(
+                out=squares[i][:], in_=roots[i][:], func=ACT.Square, scale=math.exp(-CENTRE / ROOT), bias=minus_two[:]
             )
+            nc.scalar.activation(
+                out=ratios[i][:], in_=squares[i][:], func=ACT.Exp, scale=ROOT / 2.0, bias=guess_bias[:]
+            )
+
+        def correct_log(i, part):
+            if part == 0:
+                shift[i] = work.tile([P, 4], F32, name="shift", bufs=3)
+                nc.vector.tensor_scalar(
+                    out=squares[i][:],
+                    in0=squares[i][:],
+                    scalar1=ROOT / 2.0,
+                    scalar2=math.log(M) + 1.0 - CENTRE - ROOT / 2.0,
+                    op0=ALU.mult,
+                    op1=ALU.add,
+                )
+                nc.vector.tensor_tensor(out=ratios[i][:], in0=ratios[i][:], in1=sums[i][:], op=ALU.mult)
+            if part == 1:
+                nc.vector.tensor_tensor(out=squares[i][:], in0=squares[i][:], in1=neg_max[i][:], op=ALU.add)
+            if part == 2:
+                nc.vector.tensor_tensor(out=shift[i][:], in0=squares[i][:], in1=ratios[i][:], op=ALU.subtract)
 
         def subtract(i, t, engine):
             row = neg_f[i][:, t, :]
@@ -241,18 +230,20 @@ def tile_cpclogdensityratiomatrix_x1_kernel(tc, c, w, z, out_0, out_1, out_2):
             dst = out_0[k, 512 * g : 512 * (g + 1), :].rearrange("(p t) m -> p t m", t=4)
             nc.sync.dma_start(out=dst[:, t, :], in_=row)
 
-        def pack(i, h):
-            packed[i, h] = work.tile([P, HALF, 4], BF16, name="packed", bufs=3, align_bytes=64)
-            nc.vector.tensor_copy(
-                out=packed[i, h][:],
-                in_=neg_f[i][:, :, HALF * h : HALF * (h + 1)].rearrange("p t m -> p m t"),
+        def pack(i, h, copy, c0=0, c1=HALF):
+            if c0 == 0:
+                packed[i, h] = work.tile([P, HALF, 4], BF16, name="packed", bufs=5, align_bytes=64)
+            m0 = HALF * h
+            copy(
+                out=packed[i, h][:, c0:c1, :].rearrange("p (c n) t -> p c t n", n=4),
+                in_=neg_f[i][:, :, m0 + c0 : m0 + c1].rearrange("p t (c n) -> p c t n", n=4),
             )
 
         def quantise_out(i, h):
             k, g = divmod(i, 2)
             if h == 0:
                 out_scales[i] = work.tile([P, M], U8, name="out_scales", bufs=3, align_bytes=64)
-            out_codes[i] = work.tile([P, HALF], U32, name="out_codes", bufs=4, align_bytes=64)
+            out_codes[i] = work.tile([P, HALF], U32, name="out_codes", bufs=6, align_bytes=64)
             nc.vector.quantize_mx(
                 out=out_codes[i][:].bitcast(FP8X4),
                 scales=out_scales[i][:, HALF * h : HALF * (h + 1)],
@@ -269,119 +260,131 @@ def tile_cpclogdensityratiomatrix_x1_kernel(tc, c, w, z, out_0, out_1, out_2):
                     )
 
         with tc.manual_schedule():
-            load_c(0, 2)
-            load_w(0)
+            load_w(0, 0, 256)
+            load_c(0, 0, 2)
+            load_w(0, 256, 512)
+            load_c(0, 2, 4)
             load_z(0)
-            load_c(1, 1)
+            load_c(1, 0, 4)
             for k in range(1, STEPS):
-                load_w(k)
+                load_w(k, 0, 512)
                 load_z(k)
 
+            lay_w(0, 0)
             turn(("c", 0, 0))
-            turn(("c", 0, 1))
             gather(("c", 0, 0), nc.scalar.copy)
-            gather(("c", 0, 1), nc.vector.tensor_copy)
+            lay_w(0, 1)
+            turn(("c", 0, 1))
+            gather(("c", 0, 1), nc.scalar.copy)
+            quantise_w(0)
             quantise_turned(("c", 0, 0))
             quantise_turned(("c", 0, 1))
-            lay_w(0, 0, 4)
             turn(("z", 0, 0))
-            gather(("z", 0, 0), nc.scalar.copy)
-            quantise_w(0)
+            gather(("z", 0, 0), nc.vector.tensor_copy)
             multiply_latent(0)
             round_latent(0)
             turn(("z", 0, 1))
-            gather(("z", 0, 1), nc.vector.tensor_copy)
+            gather(("z", 0, 1), nc.scalar.copy)
             multiply_latent(1)
             round_latent(1)
             quantise_turned(("z", 0, 0))
-            quantise_turned(("z", 0, 1))
-            turn(("z", 0, 2))
-            gather(("z", 0, 2), nc.scalar.copy)
             quantise_latent(0)
+            turn(("z", 0, 2))
+            quantise_turned(("z", 0, 1))
+            gather(("z", 0, 2), nc.vector.tensor_copy)
+            multiply_scores(0, 0)
             turn(("z", 0, 3))
-            gather(("z", 0, 3), nc.vector.tensor_copy)
+            gather(("z", 0, 3), nc.scalar.copy)
             multiply_latent(2)
             round_latent(2)
+            negate_and_min(0, 0)
             quantise_turned(("z", 0, 2))
-            quantise_turned(("z", 0, 3))
             quantise_latent(1)
-            multiply_scores(0)
+            quantise_turned(("z", 0, 3))
+            multiply_scores(0, 1)
+            turn(("c", 1, 0))
+            gather(("c", 1, 0), nc.scalar.copy)
+            multiply_latent(3)
+            turn(("c", 1, 1))
+            gather(("c", 1, 1), nc.scalar.copy)
 
             for s in range(TILES):
                 k, loc = divmod(s, 8)
                 banks = []
-                if s == 0:
-                    banks = [("c", 1, 0), ("c", 1, 1)]
-                elif k + 1 < STEPS and 2 <= loc < 6:
+                if k + 1 < STEPS and 2 <= loc < 6:
                     banks = [("z", k + 1, loc - 2)]
+                if s + 1 < TILES:
+                    multiply_scores(s + 1, 0)
+                    multiply_scores(s + 1, 1)
                 for key in banks:
                     turn(key)
-                if s + 3 < TILES:
-                    multiply_latent(s + 3)
-                if s + 1 < TILES:
-                    multiply_scores(s + 1)
 
-                if 1 <= s <= TILES:
+                if s > 0:
                     exponentiate(s - 1)
                 i, r = divmod(s - 4, 4)
-                if r == 0 and 0 <= i < GROUPS:
+                logs = i >= 0 and r == 0
+                if logs:
                     take_root(i)
-                    finish_log(i, nc.gpsimd)
-                for key in banks:
-                    gather(key, nc.scalar.copy)
                 if s + 3 < TILES:
                     round_latent(s + 3)
+                for key in banks:
+                    gather(key, nc.scalar.copy)
+                if logs:
+                    guess_log(i)
 
-                if s < TILES:
-                    negate_and_min(s, 0)
+                i, r = divmod(s - 5, 4)
+                logs = i >= 0 and r == 0
+                negate_and_min(s, 1)
+                if s + 1 < TILES:
+                    negate_and_min(s + 1, 0)
+                if logs:
+                    correct_log(i, 0)
                 if s + 2 < TILES:
                     quantise_latent(s + 2)
-                if s < TILES:
-                    negate_and_min(s, 1)
+                if logs:
+                    correct_log(i, 1)
                 if s == 0:
-                    for key in banks:
-                        quantise_turned(key)
+                    quantise_turned(("c", 1, 0))
+                    quantise_turned(("c", 1, 1))
                 if k + 1 < STEPS:
                     if loc < 2:
-                        lay_w(k + 1, 2 * loc, 2 * loc + 2)
+                        lay_w(k + 1, loc)
                     if loc == 2:
                         quantise_w(k + 1)
                     if 3 <= loc < 7:
                         quantise_turned(("z", k + 1, loc - 3))
-                i, r = divmod(s - 8, 4)
-                if 0 <= i < GROUPS:
-                    if r == 0:
-                        subtract(i, 0, "vector")
-                        subtract(i, 1, "scalar")
-                    if r == 1:
-                        subtract(i, 2, "scalar")
-                        subtract(i, 3, "scalar")
+                if logs:
+                    correct_log(i, 2)
+                i, r = divmod(s - 6, 4)
+                if i >= 0 and r < 3:
+                    subtract(i, r + 1, "scalar")
+                if i >= 0 and r == 0:
+                    subtract(i, 0, "vector")
+                i, r = divmod(s - 9, 4)
+                if i >= 0 and r in (0, 2):
+                    pack(i, r // 2, nc.vector.tensor_copy)
                 i, r = divmod(s - 10, 4)
-                if 0 <= i < GROUPS and r in (0, 2):
-                    pack(i, r // 2)
-                i, r = divmod(s - 11, 4)
-                if 0 <= i < GROUPS and r in (0, 2):
+                if i >= 0 and r in (0, 2):
                     quantise_out(i, r // 2)
+
+                if s + 4 < TILES:
+                    multiply_latent(s + 4)
 
             last = GROUPS - 1
             exponentiate(TILES - 1)
             take_root(last)
-            pack(last - 2, 1)
-            subtract(last - 1, 0, "vector")
-            subtract(last - 1, 1, "scalar")
-            subtract(last - 1, 2, "scalar")
+            guess_log(last)
             subtract(last - 1, 3, "vector")
             quantise_out(last - 2, 1)
-            finish_log_on_vector(last)
-            pack(last - 1, 0)
-            subtract(last, 2, "scalar")
-            subtract(last, 3, "scalar")
-            subtract(last, 0, "vector")
-            subtract(last, 1, "vector")
+            for part in range(3):
+                correct_log(last, part)
+            pack(last - 1, 0, nc.scalar.copy)
+            for t, engine in ((0, "vector"), (2, "vector"), (1, "vector"), (3, "scalar")):
+                subtract(last, t, engine)
+            pack(last, 0, nc.vector.tensor_copy)
             quantise_out(last - 1, 0)
-            pack(last - 1, 1)
-            pack(last, 0)
+            pack(last - 1, 1, nc.scalar.copy)
             quantise_out(last - 1, 1)
             quantise_out(last, 0)
-            pack(last, 1)
+            pack(last, 1, nc.scalar.copy)
             quantise_out(last, 1)

import math
from contextlib import ExitStack

import concourse.mybir as mybir
from concourse.masks import make_identity

STEPS, N, M, C, Z = 4, 1024, 1024, 512, 512
FLOPS = 2 * STEPS * N * Z * (C + M)

F32 = mybir.dt.float32
BF16 = mybir.dt.bfloat16
I32 = mybir.dt.int32
U32 = mybir.dt.uint32
U8 = mybir.dt.uint8
FP8X4 = mybir.dt.float8_e4m3fn_x4
ALU = mybir.AluOpType
ACT = mybir.ActivationFunctionType

P = 128
HALF = 512
TILES = STEPS * 8
GROUPS = STEPS * 2

ROOT = 512
CENTRE = 3.5


def tile_cpclogdensityratiomatrix_x1_kernel(tc, c, w, z, out_0, out_1, out_2):
    nc = tc.nc
    with ExitStack() as ctx:
        keep = ctx.enter_context(tc.tile_pool(name="keep", bufs=1))
        work = ctx.enter_context(tc.tile_pool(name="work", bufs=2))
        psum = ctx.enter_context(tc.psum_pool(name="psum", bufs=2))

        ident = keep.tile([P, P], F32, name="ident")
        make_identity(nc, ident[:])
        root = keep.tile([P, 4], F32, name="root")
        nc.gpsimd.memset(root[:], 1.0 / ROOT)
        minus_two = keep.tile([P, 1], F32, name="minus_two")
        nc.gpsimd.memset(minus_two[:], -2.0)
        guess_bias = keep.tile([P, 1], F32, name="guess_bias")
        nc.gpsimd.memset(guess_bias[:], -ROOT / 2.0 - CENTRE)

        c_codes = keep.tile([P, N], U32, name="c_codes", align_bytes=64)
        c_scales = keep.tile([P, N], U8, name="c_scales", align_bytes=64)
        c_raw, w_raw, z_raw = {}, {}, {}
        w_codes, w_scales, z_codes, z_scales = {}, {}, {}, {}
        turned, grouped, latent, lat_bf, lat_codes, lat_scales, w_grouped = {}, {}, {}, {}, {}, {}, {}
        scores, neg_f, first_min, neg_max, sums, shift, roots, squares, ratios = {}, {}, {}, {}, {}, {}, {}, {}, {}
        packed, out_codes, out_scales = {}, {}, {}

        def load_c(g, t0, t1):
            if t0 == 0:
                c_raw[g] = keep.tile([P, 4, C], BF16, name="c_raw%d" % g)
            src = c[512 * g : 512 * (g + 1), :].rearrange("(j t) k -> j t k", t=4)
            nc.sync.dma_start(out=c_raw[g][:, t0:t1, :], in_=src[:, t0:t1, :])

        def load_w(k, z0, z1):
            if z0 == 0:
                w_raw[k] = keep.tile([P, 4, Z], BF16, name="w_raw%d" % k)
            src = w[k].rearrange("(p j) z -> p j z", j=4)
            nc.sync.dma_start(out=w_raw[k][:, :, z0:z1], in_=src[:, :, z0:z1])

        def load_z(k):
            z_raw[k] = keep.tile([P, 8, Z], BF16, name="z_raw%d" % k)
            src = z[k].rearrange("(r j) z -> j r z", j=P)
            for r0 in (0, 4):
                nc.sync.dma_start(out=z_raw[k][:, r0 : r0 + 4, :], in_=src[:, r0 : r0 + 4, :])

        def turn(key):
            kind, i, b = key
            raw = c_raw[i] if kind == "c" else z_raw[i]
            bank = psum.tile([P, 2, 2, P], F32, name="turned", bufs=2)
            for s in range(2):
                words = raw[:, 2 * b + s, :].bitcast(F32)
                for u in range(2):
                    nc.tensor.transpose(bank[:, s, u, :], words[:, u : 256 : 2], ident[:])
            turned[key] = bank

        def gather(key, copy):
            grouped[key] = work.tile([P, 256, 4], BF16, name="grouped", bufs=4, align_bytes=64)
            dst = grouped[key][:].rearrange("p n f -> p (n f)").bitcast(F32)
            copy(
                out=dst.rearrange("p (s r u) -> p s r u", s=2, u=2),
                in_=turned.pop(key)[:].rearrange("p s u r -> p s r u"),
            )

        def quantise_turned(key):
            kind, i, b = key
            if kind == "c":
                codes, scales, at = c_codes, c_scales, 512 * i + 256 * b
            else:
                if b == 0:
                    z_codes[i] = work.tile([P, M], U32, name="z_codes", bufs=2, align_bytes=64)
                    z_scales[i] = work.tile([P, M], U8, name="z_scales", bufs=2, align_bytes=64)
                codes, scales, at = z_codes[i], z_scales[i], 256 * b
            nc.vector.quantize_mx(
                out=codes[:, at : at + 256].bitcast(FP8X4),
                scales=scales[:, at : at + 256],
                in_=grouped.pop(key)[:].rearrange("p n f -> p (n f)"),
            )

        def lay_w(k, half):
            if half == 0:
                w_grouped[k] = work.tile([P, 4 * Z], BF16, name="w_grouped", bufs=2, align_bytes=64)
            ms = slice(64 * half, 64 * half + 64)
            nc.vector.tensor_copy(
                out=w_grouped[k][:].rearrange("p (t m j) -> p t m j", t=4, j=4)[:, :, ms],
                in_=w_raw[k][:].rearrange("p j (m t) -> p t m j", t=4)[:, :, ms],
            )

        def quantise_w(k):
            w_codes[k] = work.tile([P, Z], U32, name="w_codes", bufs=2, align_bytes=64)
            w_scales[k] = work.tile([P, Z], U8, name="w_scales", bufs=2, align_bytes=64)
            nc.vector.quantize_mx(out=w_codes[k][:].bitcast(FP8X4), scales=w_scales[k][:], in_=w_grouped[k][:])

        def multiply_latent(s):
            k, rest = divmod(s, 8)
            bank = psum.tile([P, 4, P], F32, name="latent", bufs=2)
            cols = slice(P * rest, P * (rest + 1))
            for t in range(4):
                wc = slice(P * t, P * (t + 1))
                nc.tensor.matmul_mx(
                    out=bank[:, t, :],
                    lhsT=w_codes[k][:, wc].bitcast(FP8X4),
                    lhsT_scale=w_scales[k][:, wc],
                    rhs=c_codes[:, cols].bitcast(FP8X4),
                    rhs_scale=c_scales[:, cols],
                    start=True,
                    stop=True,
                )
            latent[s] = bank

        def round_latent(s):
            lat_bf[s] = work.tile([P, P, 4], BF16, name="lat_bf", bufs=4, align_bytes=64)
            nc.scalar.copy(out=lat_bf[s][:], in_=latent.pop(s)[:].rearrange("p t j -> p j t"))

        def quantise_latent(s):
            lat_codes[s] = work.tile([P, P], U32, name="lat_codes", bufs=4, align_bytes=64)
            lat_scales[s] = work.tile([P, P], U8, name="lat_scales", bufs=4, align_bytes=64)
            nc.vector.quantize_mx(
                out=lat_codes[s][:].bitcast(FP8X4),
                scales=lat_scales[s][:],
                in_=lat_bf.pop(s)[:].rearrange("p j t -> p (j t)"),
            )

        def multiply_scores(s, h):
            k = s // 8
            bank = psum.tile([P, HALF], F32, name="scores", bufs=4)
            cols = slice(HALF * h, HALF * (h + 1))
            nc.tensor.matmul_mx(
                out=bank[:],
                lhsT=lat_codes[s][:].bitcast(FP8X4),
                lhsT_scale=lat_scales[s][:],
                rhs=z_codes[k][:, cols].bitcast(FP8X4),
                rhs_scale=z_scales[k][:, cols],
                start=True,
                stop=True,
            )
            scores[s, h] = bank

        def negate_and_min(s, h):
            i, t = divmod(s, 4)
            if t == 0 and h == 0:
                neg_f[i] = work.tile([P, 4, M], F32, name="neg_f", bufs=4, align_bytes=64)
                first_min[i] = work.tile([P, 4], F32, name="first_min", bufs=2)
                neg_max[i] = work.tile([P, 4], F32, name="neg_max", bufs=3)
                sums[i] = work.tile([P, 4], F32, name="sums", bufs=3)
            nc.vector.tensor_scalar(
                out=neg_f[i][:, t, HALF * h : HALF * (h + 1)],
                in0=scores.pop((s, h))[:],
                scalar1=-1.0,
                scalar2=None if h == 0 else first_min[i][:, t : t + 1],
                op0=ALU.mult,
                op1=ALU.min,
                accum_out=(first_min if h == 0 else neg_max)[i][:, t : t + 1],
            )

        def exponentiate(s):
            i, t = divmod(s, 4)
            exps = work.tile([P, M], BF16, name="exps", bufs=2)
            nc.scalar.activation(
                out=exps[:],
                in_=neg_f[i][:, t, :],
                func=ACT.Exp,
                scale=-1.0,
                bias=neg_max[i][:, t : t + 1],
                accum_out=sums[i][:, t : t + 1],
            )

        def take_root(i):
            roots[i] = work.tile([P, 4], F32, name="roots", bufs=2)
            nc.gpsimd.tensor_tensor(out=roots[i][:], in0=sums[i][:], in1=root[:], op=ALU.pow)

        def guess_log(i):
            squares[i] = work.tile([P, 4], F32, name="squares", bufs=2)
            ratios[i] = work.tile([P, 4], F32, name="ratios", bufs=2)
            nc.scalar.activation(
                out=squares[i][:], in_=roots[i][:], func=ACT.Square, scale=math.exp(-CENTRE / ROOT), bias=minus_two[:]
            )
            nc.scalar.activation(
                out=ratios[i][:], in_=squares[i][:], func=ACT.Exp, scale=ROOT / 2.0, bias=guess_bias[:]
            )

        def correct_log(i, part):
            if part == 0:
                shift[i] = work.tile([P, 4], F32, name="shift", bufs=3)
                nc.vector.tensor_scalar(
                    out=squares[i][:],
                    in0=squares[i][:],
                    scalar1=ROOT / 2.0,
                    scalar2=math.log(M) + 1.0 - CENTRE - ROOT / 2.0,
                    op0=ALU.mult,
                    op1=ALU.add,
                )
                nc.vector.tensor_tensor(out=ratios[i][:], in0=ratios[i][:], in1=sums[i][:], op=ALU.mult)
            if part == 1:
                nc.vector.tensor_tensor(out=squares[i][:], in0=squares[i][:], in1=neg_max[i][:], op=ALU.add)
            if part == 2:
                nc.vector.tensor_tensor(out=shift[i][:], in0=squares[i][:], in1=ratios[i][:], op=ALU.subtract)

        def subtract(i, t, engine):
            row = neg_f[i][:, t, :]
            sh = shift[i][:, t : t + 1]
            if engine == "scalar":
                nc.scalar.activation(out=row, in_=row, func=ACT.Identity, scale=-1.0, bias=sh)
            else:
                nc.vector.tensor_scalar(out=row, in0=row, scalar1=-1.0, scalar2=sh, op0=ALU.mult, op1=ALU.add)
            k, g = divmod(i, 2)
            dst = out_0[k, 512 * g : 512 * (g + 1), :].rearrange("(p t) m -> p t m", t=4)
            nc.sync.dma_start(out=dst[:, t, :], in_=row)

        def pack(i, h, copy, c0=0, c1=HALF):
            if c0 == 0:
                packed[i, h] = work.tile([P, HALF, 4], BF16, name="packed", bufs=5, align_bytes=64)
            m0 = HALF * h
            copy(
                out=packed[i, h][:, c0:c1, :].rearrange("p (c n) t -> p c t n", n=4),
                in_=neg_f[i][:, :, m0 + c0 : m0 + c1].rearrange("p t (c n) -> p c t n", n=4),
            )

        def quantise_out(i, h):
            k, g = divmod(i, 2)
            if h == 0:
                out_scales[i] = work.tile([P, M], U8, name="out_scales", bufs=3, align_bytes=64)
            out_codes[i] = work.tile([P, HALF], U32, name="out_codes", bufs=6, align_bytes=64)
            nc.vector.quantize_mx(
                out=out_codes[i][:].bitcast(FP8X4),
                scales=out_scales[i][:, HALF * h : HALF * (h + 1)],
                in_=packed.pop((i, h))[:].rearrange("p m t -> p (m t)"),
            )
            m0 = M * k + HALF * h
            dst = out_1[g, :, m0 : m0 + HALF, :].rearrange("p m b -> p (m b)")
            nc.sync.dma_start(out=dst.bitcast(I32), in_=out_codes[i][:].bitcast(I32))
            if h == 1:
                for quad in range(4):
                    dst = out_2[g, 4 * quad : 4 * quad + 4, M * k : M * (k + 1)]
                    nc.sync.dma_start(
                        out=dst.bitcast(I32), in_=out_scales[i][32 * quad : 32 * quad + 4, :].bitcast(I32)
                    )

        with tc.manual_schedule():
            load_w(0, 0, 256)
            load_c(0, 0, 2)
            load_w(0, 256, 512)
            load_c(0, 2, 4)
            load_z(0)
            load_c(1, 0, 4)
            for k in range(1, STEPS):
                load_w(k, 0, 512)
                load_z(k)

            lay_w(0, 0)
            turn(("c", 0, 0))
            gather(("c", 0, 0), nc.scalar.copy)
            lay_w(0, 1)
            turn(("c", 0, 1))
            gather(("c", 0, 1), nc.scalar.copy)
            quantise_w(0)
            quantise_turned(("c", 0, 0))
            quantise_turned(("c", 0, 1))
            turn(("z", 0, 0))
            gather(("z", 0, 0), nc.vector.tensor_copy)
            multiply_latent(0)
            round_latent(0)
            turn(("z", 0, 1))
            gather(("z", 0, 1), nc.scalar.copy)
            multiply_latent(1)
            round_latent(1)
            quantise_turned(("z", 0, 0))
            quantise_latent(0)
            turn(("z", 0, 2))
            quantise_turned(("z", 0, 1))
            gather(("z", 0, 2), nc.vector.tensor_copy)
            multiply_scores(0, 0)
            turn(("z", 0, 3))
            gather(("z", 0, 3), nc.scalar.copy)
            multiply_latent(2)
            round_latent(2)
            negate_and_min(0, 0)
            quantise_turned(("z", 0, 2))
            quantise_latent(1)
            quantise_turned(("z", 0, 3))
            multiply_scores(0, 1)
            turn(("c", 1, 0))
            gather(("c", 1, 0), nc.scalar.copy)
            multiply_latent(3)
            turn(("c", 1, 1))
            gather(("c", 1, 1), nc.scalar.copy)

            for s in range(TILES):
                k, loc = divmod(s, 8)
                banks = []
                if k + 1 < STEPS and 2 <= loc < 6:
                    banks = [("z", k + 1, loc - 2)]
                if s + 1 < TILES:
                    multiply_scores(s + 1, 0)
                    multiply_scores(s + 1, 1)
                for key in banks:
                    turn(key)

                if s > 0:
                    exponentiate(s - 1)
                i, r = divmod(s - 4, 4)
                logs = i >= 0 and r == 0
                if logs:
                    take_root(i)
                if s + 3 < TILES:
                    round_latent(s + 3)
                for key in banks:
                    gather(key, nc.scalar.copy)
                if logs:
                    guess_log(i)

                i, r = divmod(s - 5, 4)
                logs = i >= 0 and r == 0
                negate_and_min(s, 1)
                if s + 1 < TILES:
                    negate_and_min(s + 1, 0)
                if logs:
                    correct_log(i, 0)
                if s + 2 < TILES:
                    quantise_latent(s + 2)
                if logs:
                    correct_log(i, 1)
                if s == 0:
                    quantise_turned(("c", 1, 0))
                    quantise_turned(("c", 1, 1))
                if k + 1 < STEPS:
                    if loc < 2:
                        lay_w(k + 1, loc)
                    if loc == 2:
                        quantise_w(k + 1)
                    if 3 <= loc < 7:
                        quantise_turned(("z", k + 1, loc - 3))
                if logs:
                    correct_log(i, 2)
                i, r = divmod(s - 6, 4)
                if i >= 0 and r < 3:
                    subtract(i, r + 1, "scalar")
                if i >= 0 and r == 0:
                    subtract(i, 0, "vector")
                i, r = divmod(s - 9, 4)
                if i >= 0 and r in (0, 2):
                    pack(i, r // 2, nc.vector.tensor_copy)
                i, r = divmod(s - 10, 4)
                if i >= 0 and r in (0, 2):
                    quantise_out(i, r // 2)

                if s + 4 < TILES:
                    multiply_latent(s + 4)

            last = GROUPS - 1
            exponentiate(TILES - 1)
            take_root(last)
            guess_log(last)
            subtract(last - 1, 3, "vector")
            quantise_out(last - 2, 1)
            for part in range(3):
                correct_log(last, part)
            pack(last - 1, 0, nc.scalar.copy)
            for t, engine in ((0, "vector"), (2, "vector"), (1, "vector"), (3, "scalar")):
                subtract(last, t, engine)
            pack(last, 0, nc.vector.tensor_copy)
            quantise_out(last - 1, 0)
            pack(last - 1, 1, nc.scalar.copy)
            quantise_out(last - 1, 1)
            quantise_out(last, 0)
            pack(last, 1, nc.scalar.copy)
            quantise_out(last, 1)
